import numpy as np
import ml_dtypes


def mxq(x, axis, fmt="e4m3"):
    dtype, down = {"e4m3": (ml_dtypes.float8_e4m3fn, 7), "e5m2": (ml_dtypes.float8_e5m2, 14)}[fmt]
    v = np.moveaxis(np.asarray(x, np.float32).astype(ml_dtypes.bfloat16).astype(np.float64), axis, -1)
    blocks = v.reshape(v.shape[:-1] + (-1, 32))
    amax = np.abs(blocks).max(-1, keepdims=True)
    byte = np.maximum(np.where(amax > 0, np.frexp(amax)[1] - 1 + 127, 0) - down, 1)
    scale = np.exp2(byte - 127.0)
    codes = (blocks / scale).astype(np.float32).astype(dtype).astype(np.float64)
    return np.moveaxis((codes * scale).reshape(v.shape), -1, axis)


WIDE = False


def mx_kscale(k):
    if not WIDE:
        return np.ones(k)
    levels = np.array([10, -10, 5, -5, 0])
    if k % 512:
        return np.exp2(np.random.permutation(np.resize(levels, k // 32))).repeat(32)
    a = np.empty((k // 512, 16))
    for p in range(k // 512):
        a[p, :8] = np.random.permutation(np.resize(levels, 8))
        for g in range(8):
            far = levels[np.abs(levels - a[p, g]) >= 10]
            a[p, g + 8] = far[np.random.randint(len(far))]
    return np.exp2(a.ravel()).repeat(32)


def f64(x):
    return np.asarray(x).astype(np.float64)


def split(x):
    m, e = np.frexp(f64(x))
    hi = np.ldexp(np.trunc(16.0 * m) / 16.0, e)
    return hi, f64(x) - hi


K, M, T = 1536, 512, 1536


def setup_inputs():
    n = np.random.standard_normal
    s = mx_kscale(K)[:, None]
    return {
        "w": (n((K, M)) / np.sqrt(K) / s).astype(np.float32),
        "x": (n((K, T)) * s).astype(np.float32),
    }


def reference(w, x):
    w_hi, w_lo = split(w)
    w_hi_, w_lo_ = mxq(w_hi, 0, "e4m3"), mxq(w_lo, 0, "e4m3")
    x_hi, x_lo = split(x)
    x_hi_, x_lo_ = mxq(x_hi, 0, "e4m3"), mxq(x_lo, 0, "e4m3")
    y = w_hi_.T @ x_hi_ + w_hi_.T @ x_lo_ + w_lo_.T @ x_hi_
    return y

@@ -1,0 +1,153 @@
+from contextlib import ExitStack
+
+import concourse.mybir as mybir
+
+K, M, T = 1536, 512, 1536
+FLOPS = 3 * 2 * K * M * T
+
+F32 = mybir.dt.float32
+BF16 = mybir.dt.bfloat16
+I32 = mybir.dt.int32
+U32 = mybir.dt.uint32
+U8 = mybir.dt.uint8
+FP8X4 = mybir.dt.float8_e4m3fn_x4
+ALU = mybir.AluOpType
+
+P = 128
+PACK = 4
+K_PASS = P * PACK
+PASSES = K // K_PASS
+M_TILES = M // P
+RUN = 4
+HI_MASK_PAIR = -0x000F0010
+
+
+def tile_mix_split3_fm_none_kernel(tc, w, x, out):
+    nc = tc.nc
+
+    pieces = [("w", 0, 0, 128), ("w", 0, 128, 128), ("w", 0, 256, 256), ("x", 0, 0, 512)]
+    pieces += [("w", 1, 0, 512), ("x", 1, 0, 512), ("w", 2, 0, 512), ("x", 2, 0, 512)]
+    pieces += [("x", c, 512, 512) for c in range(PASSES)]
+    pieces += [("x", 0, 1024, 512), ("x", 1, 1024, 512), ("x", 2, 1024, 256), ("x", 2, 1280, 256)]
+    ranges = [(0, 512), (512, 512), (1024, 256), (1280, 256)]
+
+    with ExitStack() as ctx:
+        keep = ctx.enter_context(tc.tile_pool(name="keep", bufs=1))
+        stage = ctx.enter_context(tc.tile_pool(name="stage", bufs=4))
+        results = ctx.enter_context(tc.tile_pool(name="results", bufs=6))
+        psum = ctx.enter_context(tc.psum_pool(name="psum", bufs=2))
+        ctx.enter_context(tc.manual_schedule())
+
+        codes = {}
+        scales = {}
+        for c in range(PASSES):
+            for op, width in (("w", M), ("x", T)):
+                for part in ("hi", "lo"):
+                    nm = op + part + str(c)
+                    codes[op, part, c] = keep.tile([P, width], U32, align_bytes=64, name="codes_" + nm)
+                    scales[op, part, c] = keep.tile([P, width], U8, align_bytes=64, name="scales_" + nm)
+
+        raws = []
+        for i, (op, c, col, width) in enumerate(pieces):
+            raw = keep.tile([P, PACK, width], F32, align_bytes=64, name="raw" + str(i))
+            src = w if op == "w" else x
+            rows = src[c * K_PASS : (c + 1) * K_PASS, col : col + width]
+            nc.sync.dma_start(out=raw[:], in_=rows.rearrange("(p j) w -> p j w", j=PACK))
+            raws.append(raw)
+
+        his = {}
+        los = {}
+        accs = {}
+
+        def grouped(ap):
+            return ap.rearrange("p (c i t) -> p c t i", i=RUN, t=PACK)
+
+        def copy_upper(i):
+            width = pieces[i][3]
+            hi = stage.tile([P, PACK * width], BF16, align_bytes=64, name="hi")
+            halves = raws[i][:].rearrange("p t w -> p (t w)").bitcast(BF16)[:, 1::2]
+            nc.scalar.copy(out=grouped(hi[:]), in_=halves.rearrange("p (t c i) -> p c t i", t=PACK, i=RUN))
+            his[i] = hi
+
+        def mask(i):
+            words = his[i][:].bitcast(I32)
+            nc.vector.tensor_scalar(out=words, in0=words, scalar1=HI_MASK_PAIR, scalar2=None, op0=ALU.bitwise_and)
+
+        def subtract(i):
+            width = pieces[i][3]
+            lo = stage.tile([P, PACK * width], BF16, align_bytes=64, name="lo")
+            nc.vector.tensor_tensor(
+                out=grouped(lo[:]),
+                in0=raws[i][:].rearrange("p t (c i) -> p c t i", i=RUN),
+                in1=grouped(his[i][:]),
+                op=ALU.subtract,
+            )
+            los[i] = lo
+
+        def quantize(i, part):
+            op, c, col, width = pieces[i]
+            src = his[i] if part == "hi" else los[i]
+            cols = slice(col, col + width)
+            nc.vector.quantize_mx(
+                out=codes[op, part, c][:, cols].bitcast(FP8X4),
+                scales=scales[op, part, c][:, cols],
+                in_=src[:],
+            )
+
+        def multiply(i, x_part):
+            op, c, col, width = pieces[i]
+            if op != "x":
+                return
+            for r, (n0, n) in enumerate(ranges):
+                if n0 < col or n0 >= col + width:
+                    continue
+                for m in range(M_TILES):
+                    if c == 0 and x_part == "hi":
+                        accs[r, m] = psum.tile([P, n], F32, name="acc" + str(m))
+                    for w_part in ("hi", "lo") if x_part == "hi" else ("hi",):
+                        m_cols = slice(m * P, (m + 1) * P)
+                        n_cols = slice(n0, n0 + n)
+                        nc.tensor.matmul_mx(
+                            out=accs[r, m][:],
+                            lhsT=codes["w", w_part, c][:, m_cols].bitcast(FP8X4),
+                            lhsT_scale=scales["w", w_part, c][:, m_cols],
+                            rhs=codes["x", x_part, c][:, n_cols].bitcast(FP8X4),
+                            rhs_scale=scales["x", x_part, c][:, n_cols],
+                            start=(c == 0 and x_part == "hi" and w_part == "hi"),
+                            stop=(c == PASSES - 1 and x_part == "lo"),
+                        )
+                if c == PASSES - 1 and x_part == "lo":
+                    pending.extend((r, m) for m in range(M_TILES))
+
+        pending = []
+
+        def drain(count, engines):
+            for e in range(min(count, len(pending))):
+                r, m = pending[0]
+                pending.remove((r, m))
+                n0, n = ranges[r]
+                result = results.tile([P, n], F32, name="result")
+                if engines[e % len(engines)] == "scalar":
+                    nc.scalar.copy(out=result[:], in_=accs[r, m][:])
+                else:
+                    nc.vector.tensor_copy(out=result[:], in_=accs[r, m][:])
+                nc.sync.dma_start(out=out[m * P : (m + 1) * P, n0 : n0 + n], in_=result[:])
+
+        AHEAD = 2
+        last = len(pieces) - 1
+        for i in range(AHEAD):
+            copy_upper(i)
+        for i in range(last + 2):
+            if i + AHEAD <= last:
+                copy_upper(i + AHEAD)
+            if i <= last:
+                mask(i)
+            if i >= 1:
+                quantize(i - 1, "lo")
+                multiply(i - 1, "lo")
+            if i <= last:
+                subtract(i)
+                quantize(i, "hi")
+                multiply(i, "hi")
+                drain(2, ["scalar"])
+        drain(len(pending), ["scalar", "vector"])

@@ -18,18 +18,32 @@ PACK = 4
 K_PASS = P * PACK
 PASSES = K // K_PASS
 M_TILES = M // P
-RUN = 4
+COPY_RUN = 4
+SUB_RUN = 2
+AHEAD = 2
 HI_MASK_PAIR = -0x000F0010
+
+PIECES = [
+    [("w", 0, 0, 128)],
+    [("w", 0, 128, 128)],
+    [("w", 0, 256, 256)],
+    [("x", 0, 0, 512)],
+    [("x", 0, 512, 512), ("w", 1, 0, 512)],
+    [("x", 1, 0, 512)],
+    [("x", 1, 512, 512), ("w", 2, 0, 512)],
+    [("x", 2, 0, 512)],
+    [("x", 2, 512, 512)],
+    [("x", 0, 1024, 512)],
+    [("x", 1, 1024, 256)],
+    [("x", 2, 1024, 256)],
+    [("x", 1, 1280, 256)],
+    [("x", 2, 1280, 256)],
+]
+RANGES = [(0, 512), (512, 512), (1024, 256), (1280, 256)]
 
 
 def tile_mix_split3_fm_none_kernel(tc, w, x, out):
     nc = tc.nc
-
-    pieces = [("w", 0, 0, 128), ("w", 0, 128, 128), ("w", 0, 256, 256), ("x", 0, 0, 512)]
-    pieces += [("w", 1, 0, 512), ("x", 1, 0, 512), ("w", 2, 0, 512), ("x", 2, 0, 512)]
-    pieces += [("x", c, 512, 512) for c in range(PASSES)]
-    pieces += [("x", 0, 1024, 512), ("x", 1, 1024, 512), ("x", 2, 1024, 256), ("x", 2, 1280, 256)]
-    ranges = [(0, 512), (512, 512), (1024, 256), (1280, 256)]
 
     with ExitStack() as ctx:
         keep = ctx.enter_context(tc.tile_pool(name="keep", bufs=1))
@@ -38,35 +52,44 @@ def tile_mix_split3_fm_none_kernel(tc, w, x, out):
         psum = ctx.enter_context(tc.psum_pool(name="psum", bufs=2))
         ctx.enter_context(tc.manual_schedule())
 
+        raws = []
         codes = {}
         scales = {}
-        for c in range(PASSES):
-            for op, width in (("w", M), ("x", T)):
-                for part in ("hi", "lo"):
-                    nm = op + part + str(c)
-                    codes[op, part, c] = keep.tile([P, width], U32, align_bytes=64, name="codes_" + nm)
-                    scales[op, part, c] = keep.tile([P, width], U8, align_bytes=64, name="scales_" + nm)
-
-        raws = []
-        for i, (op, c, col, width) in enumerate(pieces):
+        widths = []
+        w_place = {}
+        for i, segments in enumerate(PIECES):
+            width = sum(s[3] for s in segments)
+            widths.append(width)
             raw = keep.tile([P, PACK, width], F32, align_bytes=64, name="raw" + str(i))
-            src = w if op == "w" else x
-            rows = src[c * K_PASS : (c + 1) * K_PASS, col : col + width]
-            nc.sync.dma_start(out=raw[:], in_=rows.rearrange("(p j) w -> p j w", j=PACK))
+            offset = 0
+            for op, c, col, n in segments:
+                src = w if op == "w" else x
+                rows = src[c * K_PASS : (c + 1) * K_PASS, col : col + n]
+                nc.sync.dma_start(out=raw[:, :, offset : offset + n], in_=rows.rearrange("(p j) w -> p j w", j=PACK))
+                if op == "w":
+                    for m in range(col // P, (col + n) // P):
+                        w_place[c, m] = (i, offset + m * P - col)
+                offset += n
             raws.append(raw)
+            for part in ("hi", "lo"):
+                codes[i, part] = keep.tile([P, width], U32, align_bytes=64, name="codes_" + part + str(i))
+                scales[i, part] = keep.tile([P, width], U8, align_bytes=64, name="scales_" + part + str(i))
 
         his = {}
         los = {}
         accs = {}
+        pending = []
 
-        def grouped(ap):
-            return ap.rearrange("p (c i t) -> p c t i", i=RUN, t=PACK)
+        def grouped(ap, run):
+            return ap.rearrange("p (c i t) -> p c t i", i=run, t=PACK)
 
         def copy_upper(i):
-            width = pieces[i][3]
-            hi = stage.tile([P, PACK * width], BF16, align_bytes=64, name="hi")
+            hi = stage.tile([P, PACK * widths[i]], BF16, align_bytes=64, name="hi")
             halves = raws[i][:].rearrange("p t w -> p (t w)").bitcast(BF16)[:, 1::2]
-            nc.scalar.copy(out=grouped(hi[:]), in_=halves.rearrange("p (t c i) -> p c t i", t=PACK, i=RUN))
+            nc.scalar.copy(
+                out=grouped(hi[:], COPY_RUN),
+                in_=halves.rearrange("p (t c i) -> p c t i", t=PACK, i=COPY_RUN),
+            )
             his[i] = hi
 
         def mask(i):
@@ -74,67 +97,57 @@ def tile_mix_split3_fm_none_kernel(tc, w, x, out):
             nc.vector.tensor_scalar(out=words, in0=words, scalar1=HI_MASK_PAIR, scalar2=None, op0=ALU.bitwise_and)
 
         def subtract(i):
-            width = pieces[i][3]
-            lo = stage.tile([P, PACK * width], BF16, align_bytes=64, name="lo")
+            lo = stage.tile([P, PACK * widths[i]], BF16, align_bytes=64, name="lo")
             nc.vector.tensor_tensor(
-                out=grouped(lo[:]),
-                in0=raws[i][:].rearrange("p t (c i) -> p c t i", i=RUN),
-                in1=grouped(his[i][:]),
+                out=grouped(lo[:], SUB_RUN),
+                in0=raws[i][:].rearrange("p t (c i) -> p c t i", i=SUB_RUN),
+                in1=grouped(his[i][:], SUB_RUN),
                 op=ALU.subtract,
             )
             los[i] = lo
 
         def quantize(i, part):
-            op, c, col, width = pieces[i]
             src = his[i] if part == "hi" else los[i]
-            cols = slice(col, col + width)
-            nc.vector.quantize_mx(
-                out=codes[op, part, c][:, cols].bitcast(FP8X4),
-                scales=scales[op, part, c][:, cols],
-                in_=src[:],
-            )
+            nc.vector.quantize_mx(out=codes[i, part][:].bitcast(FP8X4), scales=scales[i, part][:], in_=src[:])
 
         def multiply(i, x_part):
-            op, c, col, width = pieces[i]
-            if op != "x":
-                return
-            for r, (n0, n) in enumerate(ranges):
-                if n0 < col or n0 >= col + width:
-                    continue
-                for m in range(M_TILES):
-                    if c == 0 and x_part == "hi":
-                        accs[r, m] = psum.tile([P, n], F32, name="acc" + str(m))
-                    for w_part in ("hi", "lo") if x_part == "hi" else ("hi",):
-                        m_cols = slice(m * P, (m + 1) * P)
-                        n_cols = slice(n0, n0 + n)
-                        nc.tensor.matmul_mx(
-                            out=accs[r, m][:],
-                            lhsT=codes["w", w_part, c][:, m_cols].bitcast(FP8X4),
-                            lhsT_scale=scales["w", w_part, c][:, m_cols],
-                            rhs=codes["x", x_part, c][:, n_cols].bitcast(FP8X4),
-                            rhs_scale=scales["x", x_part, c][:, n_cols],
-                            start=(c == 0 and x_part == "hi" and w_part == "hi"),
-                            stop=(c == PASSES - 1 and x_part == "lo"),
-                        )
-                if c == PASSES - 1 and x_part == "lo":
-                    pending.extend((r, m) for m in range(M_TILES))
+            offset = 0
+            for op, c, col, width in PIECES[i]:
+                for r, (n0, n) in enumerate(RANGES):
+                    if op == "w" or n0 < col or n0 >= col + width:
+                        continue
+                    n_cols = slice(offset + n0 - col, offset + n0 - col + n)
+                    for m in range(M_TILES):
+                        if c == 0 and x_part == "hi":
+                            accs[r, m] = psum.tile([P, n], F32, name="acc" + str(m))
+                        j, m0 = w_place[c, m]
+                        m_cols = slice(m0, m0 + P)
+                        for w_part in ("hi", "lo") if x_part == "hi" else ("hi",):
+                            nc.tensor.matmul_mx(
+                                out=accs[r, m][:],
+                                lhsT=codes[j, w_part][:, m_cols].bitcast(FP8X4),
+                                lhsT_scale=scales[j, w_part][:, m_cols],
+                                rhs=codes[i, x_part][:, n_cols].bitcast(FP8X4),
+                                rhs_scale=scales[i, x_part][:, n_cols],
+                                start=(c == 0 and x_part == "hi" and w_part == "hi"),
+                                stop=(c == PASSES - 1 and x_part == "lo"),
+                            )
+                    if c == PASSES - 1 and x_part == "lo":
+                        pending.extend((r, m) for m in range(M_TILES))
+                offset += width
 
-        pending = []
-
-        def drain(count, engines):
-            for e in range(min(count, len(pending))):
-                r, m = pending[0]
-                pending.remove((r, m))
-                n0, n = ranges[r]
+        def drain(with_vector):
+            for r, m in pending:
+                n0, n = RANGES[r]
                 result = results.tile([P, n], F32, name="result")
-                if engines[e % len(engines)] == "scalar":
-                    nc.scalar.copy(out=result[:], in_=accs[r, m][:])
-                else:
+                if with_vector and m % 2 == 1:
                     nc.vector.tensor_copy(out=result[:], in_=accs[r, m][:])
+                else:
+                    nc.scalar.copy(out=result[:], in_=accs[r, m][:])
                 nc.sync.dma_start(out=out[m * P : (m + 1) * P, n0 : n0 + n], in_=result[:])
+            pending.clear()
 
-        AHEAD = 2
-        last = len(pieces) - 1
+        last = len(PIECES) - 1
         for i in range(AHEAD):
             copy_upper(i)
         for i in range(last + 2):
@@ -145,9 +158,8 @@ def tile_mix_split3_fm_none_kernel(tc, w, x, out):
             if i >= 1:
                 quantize(i - 1, "lo")
                 multiply(i - 1, "lo")
+            drain(with_vector=(i > last))
             if i <= last:
                 subtract(i)
                 quantize(i, "hi")
                 multiply(i, "hi")
-                drain(2, ["scalar"])
-        drain(len(pending), ["scalar", "vector"])

@@ -19,25 +19,24 @@ K_PASS = P * PACK
 PASSES = K // K_PASS
 M_TILES = M // P
 COPY_RUN = 4
-SUB_RUN = 2
+SUB_RUN = 4
 AHEAD = 2
 HI_MASK_PAIR = -0x000F0010
 
-PIECES = [
-    [("w", 0, 0, 128)],
-    [("w", 0, 128, 128)],
-    [("w", 0, 256, 256)],
-    [("x", 0, 0, 512)],
-    [("x", 0, 512, 512), ("w", 1, 0, 512)],
-    [("x", 1, 0, 512)],
-    [("x", 1, 512, 512), ("w", 2, 0, 512)],
-    [("x", 2, 0, 512)],
-    [("x", 2, 512, 512)],
-    [("x", 0, 1024, 512)],
-    [("x", 1, 1024, 256)],
-    [("x", 2, 1024, 256)],
-    [("x", 1, 1280, 256)],
-    [("x", 2, 1280, 256)],
+BLOCKS = [
+    ([("w", 0, 0, 512)], [128, 128, 256]),
+    ([("x", 0, 0, 512)], [256, 256]),
+    ([("x", 0, 512, 512)], [512]),
+    ([("w", 1, 0, 512)], [512]),
+    ([("x", 1, 0, 512)], [512]),
+    ([("x", 1, 512, 512), ("w", 2, 0, 512)], [1024]),
+    ([("x", 2, 0, 512)], [512]),
+    ([("x", 2, 512, 512)], [512]),
+    ([("x", 0, 1024, 512)], [512]),
+    ([("x", 1, 1024, 256)], [256]),
+    ([("x", 2, 1024, 256)], [256]),
+    ([("x", 1, 1280, 256)], [256]),
+    ([("x", 2, 1280, 256)], [256]),
 ]
 RANGES = [(0, 512), (512, 512), (1024, 256), (1280, 256)]
 
@@ -55,25 +54,34 @@ def tile_mix_split3_fm_none_kernel(tc, w, x, out):
         raws = []
         codes = {}
         scales = {}
-        widths = []
         w_place = {}
-        for i, segments in enumerate(PIECES):
-            width = sum(s[3] for s in segments)
-            widths.append(width)
-            raw = keep.tile([P, PACK, width], F32, align_bytes=64, name="raw" + str(i))
-            offset = 0
-            for op, c, col, n in segments:
-                src = w if op == "w" else x
-                rows = src[c * K_PASS : (c + 1) * K_PASS, col : col + n]
-                nc.sync.dma_start(out=raw[:, :, offset : offset + n], in_=rows.rearrange("(p j) w -> p j w", j=PACK))
-                if op == "w":
-                    for m in range(col // P, (col + n) // P):
-                        w_place[c, m] = (i, offset + m * P - col)
-                offset += n
+        steps = []
+        for b, (segments, cuts) in enumerate(BLOCKS):
+            width = sum(cuts)
+            raw = keep.tile([P, PACK, width], F32, align_bytes=64, name="raw" + str(b))
             raws.append(raw)
             for part in ("hi", "lo"):
-                codes[i, part] = keep.tile([P, width], U32, align_bytes=64, name="codes_" + part + str(i))
-                scales[i, part] = keep.tile([P, width], U8, align_bytes=64, name="scales_" + part + str(i))
+                codes[b, part] = keep.tile([P, width], U32, align_bytes=64, name="codes_" + part + str(b))
+                scales[b, part] = keep.tile([P, width], U8, align_bytes=64, name="scales_" + part + str(b))
+            first = 0
+            for cut in cuts:
+                done = []
+                offset = 0
+                for op, c, col, n in segments:
+                    lo_col = max(first, offset)
+                    hi_col = min(first + cut, offset + n)
+                    if lo_col < hi_col:
+                        src = w if op == "w" else x
+                        rows = src[c * K_PASS : (c + 1) * K_PASS, col + lo_col - offset : col + hi_col - offset]
+                        nc.sync.dma_start(out=raw[:, :, lo_col:hi_col], in_=rows.rearrange("(p j) w -> p j w", j=PACK))
+                        if hi_col == offset + n:
+                            done.append((op, c, col, n, offset))
+                    if op == "w":
+                        for m in range(col // P, (col + n) // P):
+                            w_place[c, m] = (b, offset + m * P - col)
+                    offset += n
+                steps.append((b, first, cut, done))
+                first += cut
 
         his = {}
         los = {}
@@ -84,11 +92,12 @@ def tile_mix_split3_fm_none_kernel(tc, w, x, out):
             return ap.rearrange("p (c i t) -> p c t i", i=run, t=PACK)
 
         def copy_upper(i):
-            hi = stage.tile([P, PACK * widths[i]], BF16, align_bytes=64, name="hi")
-            halves = raws[i][:].rearrange("p t w -> p (t w)").bitcast(BF16)[:, 1::2]
+            b, first, width, done = steps[i]
+            hi = stage.tile([P, PACK * width], BF16, align_bytes=64, name="hi")
+            halves = raws[b][:].bitcast(BF16)[:, :, 2 * first + 1 : 2 * (first + width) : 2]
             nc.scalar.copy(
                 out=grouped(hi[:], COPY_RUN),
-                in_=halves.rearrange("p (t c i) -> p c t i", t=PACK, i=COPY_RUN),
+                in_=halves.rearrange("p t (c i) -> p c t i", i=COPY_RUN),
             )
             his[i] = hi
 
@@ -97,22 +106,25 @@ def tile_mix_split3_fm_none_kernel(tc, w, x, out):
             nc.vector.tensor_scalar(out=words, in0=words, scalar1=HI_MASK_PAIR, scalar2=None, op0=ALU.bitwise_and)
 
         def subtract(i):
-            lo = stage.tile([P, PACK * widths[i]], BF16, align_bytes=64, name="lo")
+            b, first, width, done = steps[i]
+            lo = stage.tile([P, PACK * width], BF16, align_bytes=64, name="lo")
             nc.vector.tensor_tensor(
                 out=grouped(lo[:], SUB_RUN),
-                in0=raws[i][:].rearrange("p t (c i) -> p c t i", i=SUB_RUN),
+                in0=raws[b][:, :, first : first + width].rearrange("p t (c i) -> p c t i", i=SUB_RUN),
                 in1=grouped(his[i][:], SUB_RUN),
                 op=ALU.subtract,
             )
             los[i] = lo
 
         def quantize(i, part):
+            b, first, width, done = steps[i]
             src = his[i] if part == "hi" else los[i]
-            nc.vector.quantize_mx(out=codes[i, part][:].bitcast(FP8X4), scales=scales[i, part][:], in_=src[:])
+            cols = slice(first, first + width)
+            nc.vector.quantize_mx(out=codes[b, part][:, cols].bitcast(FP8X4), scales=scales[b, part][:, cols], in_=src[:])
 
         def multiply(i, x_part):
-            offset = 0
-            for op, c, col, width in PIECES[i]:
+            b = steps[i][0]
+            for op, c, col, width, offset in steps[i][3]:
                 for r, (n0, n) in enumerate(RANGES):
                     if op == "w" or n0 < col or n0 >= col + width:
                         continue
@@ -127,14 +139,13 @@ def tile_mix_split3_fm_none_kernel(tc, w, x, out):
                                 out=accs[r, m][:],
                                 lhsT=codes[j, w_part][:, m_cols].bitcast(FP8X4),
                                 lhsT_scale=scales[j, w_part][:, m_cols],
-                                rhs=codes[i, x_part][:, n_cols].bitcast(FP8X4),
-                                rhs_scale=scales[i, x_part][:, n_cols],
+                                rhs=codes[b, x_part][:, n_cols].bitcast(FP8X4),
+                                rhs_scale=scales[b, x_part][:, n_cols],
                                 start=(c == 0 and x_part == "hi" and w_part == "hi"),
                                 stop=(c == PASSES - 1 and x_part == "lo"),
                             )
                     if c == PASSES - 1 and x_part == "lo":
                         pending.extend((r, m) for m in range(M_TILES))
-                offset += width
 
         def drain(with_vector):
             for r, m in pending:
@@ -147,19 +158,22 @@ def tile_mix_split3_fm_none_kernel(tc, w, x, out):
                 nc.sync.dma_start(out=out[m * P : (m + 1) * P, n0 : n0 + n], in_=result[:])
             pending.clear()
 
-        last = len(PIECES) - 1
+        last = len(steps) - 1
         for i in range(AHEAD):
             copy_upper(i)
+        mask(0)
         for i in range(last + 2):
             if i + AHEAD <= last:
                 copy_upper(i + AHEAD)
-            if i <= last:
-                mask(i)
             if i >= 1:
                 quantize(i - 1, "lo")
                 multiply(i - 1, "lo")
             drain(with_vector=(i > last))
             if i <= last:
                 subtract(i)
+                if 3 <= i < last:
+                    mask(i + 1)
                 quantize(i, "hi")
                 multiply(i, "hi")
+                if i < min(3, last):
+                    mask(i + 1)

@@ -19,7 +19,7 @@ K_PASS = P * PACK
 PASSES = K // K_PASS
 M_TILES = M // P
 COPY_RUN = 4
-SUB_RUN = 4
+SUB_RUN = 2
 AHEAD = 2
 HI_MASK_PAIR = -0x000F0010
 

from contextlib import ExitStack

import concourse.mybir as mybir

K, M, T = 1536, 512, 1536
FLOPS = 3 * 2 * K * M * T

F32 = mybir.dt.float32
BF16 = mybir.dt.bfloat16
I32 = mybir.dt.int32
U32 = mybir.dt.uint32
U8 = mybir.dt.uint8
FP8X4 = mybir.dt.float8_e4m3fn_x4
ALU = mybir.AluOpType

P = 128
PACK = 4
K_PASS = P * PACK
PASSES = K // K_PASS
M_TILES = M // P
COPY_RUN = 4
SUB_RUN = 2
AHEAD = 2
HI_MASK_PAIR = -0x000F0010

BLOCKS = [
    ([("w", 0, 0, 512)], [128, 128, 256]),
    ([("x", 0, 0, 512)], [256, 256]),
    ([("x", 0, 512, 512)], [512]),
    ([("w", 1, 0, 512)], [512]),
    ([("x", 1, 0, 512)], [512]),
    ([("x", 1, 512, 512), ("w", 2, 0, 512)], [1024]),
    ([("x", 2, 0, 512)], [512]),
    ([("x", 2, 512, 512)], [512]),
    ([("x", 0, 1024, 512)], [512]),
    ([("x", 1, 1024, 256)], [256]),
    ([("x", 2, 1024, 256)], [256]),
    ([("x", 1, 1280, 256)], [256]),
    ([("x", 2, 1280, 256)], [256]),
]
RANGES = [(0, 512), (512, 512), (1024, 256), (1280, 256)]


def tile_mix_split3_fm_none_kernel(tc, w, x, out):
    nc = tc.nc

    with ExitStack() as ctx:
        keep = ctx.enter_context(tc.tile_pool(name="keep", bufs=1))
        stage = ctx.enter_context(tc.tile_pool(name="stage", bufs=4))
        results = ctx.enter_context(tc.tile_pool(name="results", bufs=6))
        psum = ctx.enter_context(tc.psum_pool(name="psum", bufs=2))
        ctx.enter_context(tc.manual_schedule())

        raws = []
        codes = {}
        scales = {}
        w_place = {}
        steps = []
        for b, (segments, cuts) in enumerate(BLOCKS):
            width = sum(cuts)
            raw = keep.tile([P, PACK, width], F32, align_bytes=64, name="raw" + str(b))
            raws.append(raw)
            for part in ("hi", "lo"):
                codes[b, part] = keep.tile([P, width], U32, align_bytes=64, name="codes_" + part + str(b))
                scales[b, part] = keep.tile([P, width], U8, align_bytes=64, name="scales_" + part + str(b))
            first = 0
            for cut in cuts:
                done = []
                offset = 0
                for op, c, col, n in segments:
                    lo_col = max(first, offset)
                    hi_col = min(first + cut, offset + n)
                    if lo_col < hi_col:
                        src = w if op == "w" else x
                        rows = src[c * K_PASS : (c + 1) * K_PASS, col + lo_col - offset : col + hi_col - offset]
                        nc.sync.dma_start(out=raw[:, :, lo_col:hi_col], in_=rows.rearrange("(p j) w -> p j w", j=PACK))
                        if hi_col == offset + n:
                            done.append((op, c, col, n, offset))
                    if op == "w":
                        for m in range(col // P, (col + n) // P):
                            w_place[c, m] = (b, offset + m * P - col)
                    offset += n
                steps.append((b, first, cut, done))
                first += cut

        his = {}
        los = {}
        accs = {}
        pending = []

        def grouped(ap, run):
            return ap.rearrange("p (c i t) -> p c t i", i=run, t=PACK)

        def copy_upper(i):
            b, first, width, done = steps[i]
            hi = stage.tile([P, PACK * width], BF16, align_bytes=64, name="hi")
            halves = raws[b][:].bitcast(BF16)[:, :, 2 * first + 1 : 2 * (first + width) : 2]
            nc.scalar.copy(
                out=grouped(hi[:], COPY_RUN),
                in_=halves.rearrange("p t (c i) -> p c t i", i=COPY_RUN),
            )
            his[i] = hi

        def mask(i):
            words = his[i][:].bitcast(I32)
            nc.vector.tensor_scalar(out=words, in0=words, scalar1=HI_MASK_PAIR, scalar2=None, op0=ALU.bitwise_and)

        def subtract(i):
            b, first, width, done = steps[i]
            lo = stage.tile([P, PACK * width], BF16, align_bytes=64, name="lo")
            nc.vector.tensor_tensor(
                out=grouped(lo[:], SUB_RUN),
                in0=raws[b][:, :, first : first + width].rearrange("p t (c i) -> p c t i", i=SUB_RUN),
                in1=grouped(his[i][:], SUB_RUN),
                op=ALU.subtract,
            )
            los[i] = lo

        def quantize(i, part):
            b, first, width, done = steps[i]
            src = his[i] if part == "hi" else los[i]
            cols = slice(first, first + width)
            nc.vector.quantize_mx(out=codes[b, part][:, cols].bitcast(FP8X4), scales=scales[b, part][:, cols], in_=src[:])

        def multiply(i, x_part):
            b = steps[i][0]
            for op, c, col, width, offset in steps[i][3]:
                for r, (n0, n) in enumerate(RANGES):
                    if op == "w" or n0 < col or n0 >= col + width:
                        continue
                    n_cols = slice(offset + n0 - col, offset + n0 - col + n)
                    for m in range(M_TILES):
                        if c == 0 and x_part == "hi":
                            accs[r, m] = psum.tile([P, n], F32, name="acc" + str(m))
                        j, m0 = w_place[c, m]
                        m_cols = slice(m0, m0 + P)
                        for w_part in ("hi", "lo") if x_part == "hi" else ("hi",):
                            nc.tensor.matmul_mx(
                                out=accs[r, m][:],
                                lhsT=codes[j, w_part][:, m_cols].bitcast(FP8X4),
                                lhsT_scale=scales[j, w_part][:, m_cols],
                                rhs=codes[b, x_part][:, n_cols].bitcast(FP8X4),
                                rhs_scale=scales[b, x_part][:, n_cols],
                                start=(c == 0 and x_part == "hi" and w_part == "hi"),
                                stop=(c == PASSES - 1 and x_part == "lo"),
                            )
                    if c == PASSES - 1 and x_part == "lo":
                        pending.extend((r, m) for m in range(M_TILES))

        def drain(with_vector):
            for r, m in pending:
                n0, n = RANGES[r]
                result = results.tile([P, n], F32, name="result")
                if with_vector and m % 2 == 1:
                    nc.vector.tensor_copy(out=result[:], in_=accs[r, m][:])
                else:
                    nc.scalar.copy(out=result[:], in_=accs[r, m][:])
                nc.sync.dma_start(out=out[m * P : (m + 1) * P, n0 : n0 + n], in_=result[:])
            pending.clear()

        last = len(steps) - 1
        for i in range(AHEAD):
            copy_upper(i)
        mask(0)
        for i in range(last + 2):
            if i + AHEAD <= last:
                copy_upper(i + AHEAD)
            if i >= 1:
                quantize(i - 1, "lo")
                multiply(i - 1, "lo")
            drain(with_vector=(i > last))
            if i <= last:
                subtract(i)
                if 3 <= i < last:
                    mask(i + 1)
                quantize(i, "hi")
                multiply(i, "hi")
                if i < min(3, last):
                    mask(i + 1)
